import numpy as np
import ml_dtypes


def mxq(x, axis, fmt="e4m3"):
    dtype, down = {"e4m3": (ml_dtypes.float8_e4m3fn, 7), "e5m2": (ml_dtypes.float8_e5m2, 14)}[fmt]
    v = np.moveaxis(np.asarray(x, np.float32).astype(ml_dtypes.bfloat16).astype(np.float64), axis, -1)
    blocks = v.reshape(v.shape[:-1] + (-1, 32))
    amax = np.abs(blocks).max(-1, keepdims=True)
    byte = np.maximum(np.where(amax > 0, np.frexp(amax)[1] - 1 + 127, 0) - down, 1)
    scale = np.exp2(byte - 127.0)
    codes = (blocks / scale).astype(np.float32).astype(dtype).astype(np.float64)
    return np.moveaxis((codes * scale).reshape(v.shape), -1, axis)


WIDE = False


def mx_kscale(k):
    if not WIDE:
        return np.ones(k)
    levels = np.array([10, -10, 5, -5, 0])
    if k % 512:
        return np.exp2(np.random.permutation(np.resize(levels, k // 32))).repeat(32)
    a = np.empty((k // 512, 16))
    for p in range(k // 512):
        a[p, :8] = np.random.permutation(np.resize(levels, 8))
        for g in range(8):
            far = levels[np.abs(levels - a[p, g]) >= 10]
            a[p, g + 8] = far[np.random.randint(len(far))]
    return np.exp2(a.ravel()).repeat(32)


def f64(x):
    return np.asarray(x).astype(np.float64)


def striped(idx):
    return np.tile(np.asarray(idx).reshape(-1, 16).T, (8, 1)).astype(np.uint16)


def unstriped(offs):
    return offs[:16].T.reshape(-1).astype(np.int64)


E2M1 = np.array([0.0, 0.5, 1.0, 1.5, 2.0, 3.0, 4.0, 6.0, -0.0, -0.5, -1.0, -1.5, -2.0, -3.0, -4.0, -6.0])


def pack_weight(w, fmt):
    k, n = w.shape
    w = f64(np.asarray(w, np.float32).astype(ml_dtypes.bfloat16)).reshape(k // 32, 32, n)
    amax = np.abs(w).max(1)
    if fmt == "e4m3":
        byte = np.frexp(amax)[1] - 1 + 127 - 7
    else:
        mant, ex = np.frexp(amax / 6.0)
        byte = np.where(mant > 0.5, ex, ex - 1) + 127
    byte = np.clip(np.where(amax > 0, byte, 1), 1, 254)
    scaled = (w * np.exp2(127.0 - byte)[:, None, :]).reshape(k, n).astype(np.float32)
    by_word = np.ascontiguousarray(scaled.reshape(k // 512, 128, 4, n).transpose(0, 1, 3, 2))
    if fmt == "e4m3":
        words = by_word.astype(ml_dtypes.float8_e4m3fn).view(np.uint8)
    else:
        c = by_word.astype(ml_dtypes.float4_e2m1fn).view(np.uint8) & 0xF
        words = (c[..., 0::2] | (c[..., 1::2] << 4)).reshape(k // 512, 128, 2 * n)
    return np.ascontiguousarray(words), np.ascontiguousarray(byte.astype(np.uint8).reshape(k // 512, 16, n))


def unpack_weight(words, scales, fmt):
    g, _, n = scales.shape
    words = np.ascontiguousarray(words).reshape(g, 128, n, -1)
    if fmt == "e4m3":
        vals = words.view(ml_dtypes.float8_e4m3fn).astype(np.float64)
    else:
        nib = np.empty((g, 128, n, 4), np.uint8)
        nib[..., 0::2] = words & 0xF
        nib[..., 1::2] = words >> 4
        vals = E2M1[nib]
    vals = vals * np.repeat(np.exp2(scales.astype(np.float64) - 127.0), 8, axis=1)[..., None]
    return vals.transpose(0, 1, 3, 2).reshape(g * 512, n)


def softplus(v):
    return np.log(1.0 + np.exp(v))


K, T, J, N = 1024, 2048, 512, 512


def setup_inputs():
    n = np.random.standard_normal
    idx = np.random.permutation(T)[:J]
    idx2 = np.random.permutation(T)[:J]
    fk = mx_kscale(K)
    xtp = pack_weight(n((K, T)) / fk[:, None], "e4m3")
    wap = pack_weight(n((K, N)) * 1 / np.sqrt(K) * fk[:, None], "e2m1")
    return {
        "xt_words": xtp[0],
        "xt_scales": xtp[1],
        "wa_words": wap[0],
        "wa_scales": wap[1],
        "wb": (n((K, N)) * 1 / np.sqrt(K) * fk[:, None]).astype(np.float32),
        "gm": (np.random.uniform(0.5, 2.0, (N, 1))).astype(np.float32),
        "offs": striped(idx),
        "offs2": striped(idx2),
    }


def reference(xt_words, xt_scales, wa_words, wa_scales, wb, gm, offs, offs2):
    idx = unstriped(offs)
    idx2 = unstriped(offs2)
    xtu = unpack_weight(xt_words, xt_scales, "e4m3")
    wau = unpack_weight(wa_words, wa_scales, "e2m1")
    xtidxg = xtu[:, idx]
    p = wau.T @ xtidxg
    wbq = mxq(f64(wb), 0, "e4m3")
    xtidx2g = xtu[:, idx2]
    q = wbq.T @ xtidx2g
    y = f64(gm) * softplus(np.abs(p - q))
    return y

from contextlib import ExitStack

import concourse.mybir as mybir

K, T, J, N = 1024, 2048, 512, 512
FLOPS = 2 * 2 * K * N * J

F32 = mybir.dt.float32
BF16 = mybir.dt.bfloat16
I32 = mybir.dt.int32
U32 = mybir.dt.uint32
U16 = mybir.dt.uint16
U8 = mybir.dt.uint8
FP8X4 = mybir.dt.float8_e4m3fn_x4
FP4X4 = mybir.dt.float4_e2m1fn_x4
ACT = mybir.ActivationFunctionType
ALU = mybir.AluOpType

P = 128
PACK = 4
PASSES = K // (P * PACK)
QUADS = 4
ROWS = 4
TILES = N // P


def tile_list_gap_of_two_picks_kernel(tc, xt_words, xt_scales, wa_words, wa_scales, wb, gm, offs, offs2, out):
    nc = tc.nc
    with ExitStack() as ctx:
        keep = ctx.enter_context(tc.tile_pool(name="keep", bufs=1))
        psum = ctx.enter_context(tc.psum_pool(name="psum", bufs=1))

        lists = [keep.tile([P, J // 16], U16, name=f"list{i}") for i in range(2)]
        x_scale = keep.tile([P, T], U8, align_bytes=64)
        x_words = [keep.tile([P, T], U32, name=f"x_words{z}", align_bytes=64) for z in range(PASSES)]
        wa_codes = keep.tile([P, PASSES, 2 * N], U8, align_bytes=64)
        wa_scale = keep.tile([P, PASSES, N], U8, align_bytes=64)
        moved_scale = keep.tile([P, J], U8, align_bytes=64)
        gain = keep.tile([P, TILES], F32)

        nc.vector.memset(x_scale[:].bitcast(I32), 0)
        nc.vector.memset(wa_scale[:].rearrange("p z n -> p (z n)").bitcast(I32), 0)
        nc.gpsimd.memset(moved_scale[:].bitcast(I32), 0)

        nc.sync.dma_start(lists[0][:], offs)
        nc.sync.dma_start(lists[1][:], offs2)
        nc.sync.dma_start(wa_codes[:].bitcast(I32), wa_words.rearrange("z p c -> p z c").bitcast(I32))
        for q in range(QUADS):
            nc.sync.dma_start(
                x_scale[32 * q : 32 * q + PASSES * ROWS, :].bitcast(I32),
                xt_scales[:, ROWS * q : ROWS * (q + 1), :].bitcast(I32),
            )
        for z in range(PASSES):
            nc.sync.dma_start(x_words[z][:].bitcast(I32), xt_words[z].rearrange("p t r -> p (t r)").bitcast(I32))
        for q in range(QUADS):
            nc.sync.dma_start(
                wa_scale[32 * q : 32 * q + ROWS, :, :].bitcast(I32),
                wa_scales[:, ROWS * q : ROWS * (q + 1), :].rearrange("z r c -> r z c").bitcast(I32),
            )

        wb_raw = {}
        for t in range(TILES):
            for z in range(PASSES):
                wb_raw[t, z] = keep.tile([P, PACK, P], F32, name=f"wb_raw{t}_{z}")
                rows = wb[z * P * PACK : (z + 1) * P * PACK, t * P : (t + 1) * P]
                nc.sync.dma_start(wb_raw[t, z][:], rows.rearrange("(p r) n -> p r n", r=PACK))
        with nc.allow_non_contiguous_dma(reason="one gain for each partition"):
            nc.sync.dma_start(gain[:], gm.rearrange("(t p) o -> p (t o)", p=P))

        picked_scale = []
        for i in range(2):
            g = keep.tile([P, J], U8, name=f"picked_scale{i}", align_bytes=64)
            nc.vector.tensor_copy(g[:], x_scale[:].indirect(lists[i][:]))
            picked_scale.append(g)
        span = 32 * (QUADS - 1) + ROWS
        nc.gpsimd.dma_start(moved_scale[0:span, :].bitcast(I32), picked_scale[0][ROWS : ROWS + span, :].bitcast(I32))
        picked = {}
        for z in range(PASSES):
            for i in range(2):
                picked[i, z] = keep.tile([P, J], U32, name=f"picked{i}_{z}", align_bytes=64)
                nc.vector.tensor_copy(picked[i, z][:], x_words[z][:].indirect(lists[i][:]))
        first_scale = [picked_scale[0][:], moved_scale[:]]
        second_scale = [picked_scale[1][ROWS * z : P, :] for z in range(PASSES)]

        gap = keep.tile([P, TILES, J], F32)
        decay = keep.tile([P, TILES, J], F32)
        linear = keep.tile([P, TILES, J], F32)
        logs = keep.tile([P, TILES, J], F32)
        width = J // TILES
        last_gain = keep.tile([P, 2], F32)
        nc.gpsimd.tensor_scalar(last_gain[:, 0:1], gain[:, TILES - 1 : TILES], 2.0, None, ALU.mult)
        nc.gpsimd.tensor_scalar(last_gain[:, 1:2], gain[:, TILES - 1 : TILES], -1.0, None, ALU.mult)
        banks = [psum.tile([P, J], F32, name=f"bank{t}") for t in range(TILES)]
        for z in range(PASSES):
            for t in range(TILES):
                nc.tensor.matmul_mx(
                    out=banks[t][:],
                    lhsT=wa_codes[:, z, 2 * t * P : 2 * (t + 1) * P].bitcast(FP4X4),
                    lhsT_scale=wa_scale[:, z, t * P : (t + 1) * P],
                    rhs=picked[0, z][:].bitcast(FP8X4),
                    rhs_scale=first_scale[z],
                    start=(z == 0),
                    stop=False,
                )
        for t in range(TILES):
            bank = banks[t]
            woven = keep.tile([P, PASSES, P, PACK], BF16, name=f"woven{t}", align_bytes=64)
            for z in range(PASSES):
                dst = woven[:, z].rearrange("p (c i) r -> p c r i", i=4)
                src = wb_raw[t, z][:].rearrange("p r (c i) -> p c r i", i=4)
                if t < 2:
                    nc.scalar.activation(dst, src, ACT.Copy, scale=-1.0)
                else:
                    nc.vector.tensor_scalar(dst, src, -1.0, None, ALU.mult)
            codes = keep.tile([P, PASSES, P], U32, name=f"wb_codes{t}", align_bytes=64)
            scale = keep.tile([P, PASSES, P], U8, name=f"wb_scale{t}", align_bytes=64)
            if t < TILES - 1:
                nc.vector.quantize_mx(
                    out=codes[:].rearrange("p z n -> p (z n)").bitcast(FP8X4),
                    scales=scale[:].rearrange("p z n -> p (z n)"),
                    in_=woven[:].rearrange("p z n r -> p (z n r)"),
                )
            else:
                for z in range(PASSES):
                    nc.vector.quantize_mx(
                        out=codes[:, z].bitcast(FP8X4), scales=scale[:, z], in_=woven[:, z].rearrange("p n r -> p (n r)")
                    )
            for z in range(PASSES):
                nc.tensor.matmul_mx(
                    out=bank[:],
                    lhsT=codes[:, z].bitcast(FP8X4),
                    lhsT_scale=scale[:, z],
                    rhs=picked[1, z][:].bitcast(FP8X4),
                    rhs_scale=second_scale[z],
                    start=False,
                    stop=(z == PASSES - 1),
                )
            if t < TILES - 1:
                nc.scalar.activation(gap[:, t, :], bank[:], ACT.Abs)
                nc.scalar.activation(decay[:, t, :], gap[:, t, :], ACT.Exp, scale=-1.0)
                nc.vector.tensor_scalar(linear[:, t, :], gap[:, t, :], gain[:, t : t + 1], None, ALU.mult)
            else:
                parked = logs[:, :, 0:width]
                nc.scalar.activation(parked, bank[:].rearrange("p (a b) -> p a b", b=width), ACT.Tanh, scale=0.5)
                nc.vector.scalar_tensor_tensor(
                    decay[:, t, :].rearrange("p (a b) -> p a b", b=width), parked, -1.0, parked, ALU.mult, ALU.max
                )
                nc.vector.tensor_scalar(gap[:, t, :], bank[:], 0.0, last_gain[:, 0:1], ALU.max, ALU.mult)
                nc.vector.scalar_tensor_tensor(
                    linear[:, t, :], bank[:], last_gain[:, 1:2], gap[:, t, :], ALU.mult, ALU.add
                )

        pieces = [(t, 0, J) for t in range(TILES - 1)] + [(TILES - 1, 0, J // 2), (TILES - 1, J // 2, J)]
        for t, lo, hi in pieces:
            result = keep.tile([P, hi - lo], F32, name=f"result{t}_{lo}")
            if t < TILES - 1:
                nc.scalar.activation(logs[:, t, lo:hi], decay[:, t, lo:hi], ACT.Ln, bias=1.0)
                factor = gain[:, t : t + 1]
            else:
                nc.scalar.activation(logs[:, t, lo:hi], decay[:, t, lo:hi], ACT.Ln, bias=0.5, scale=0.5)
                factor = last_gain[:, 1:2]
            nc.vector.scalar_tensor_tensor(result[:], logs[:, t, lo:hi], factor, linear[:, t, lo:hi], ALU.mult, ALU.add)
            nc.sync.dma_start(out[t * P : (t + 1) * P, lo:hi], result[:])
